import numpy as np, ml_dtypes
CORES = [23,119,17,113]
N = 4
import mx_ref
BF = ml_dtypes.bfloat16
def gentries(a):
    return np.ascontiguousarray(a.reshape(8, 16, -1).transpose(0, 2, 1)).reshape(8, -1)
def gtable(e):
    e = np.asarray(e); return np.ascontiguousarray(e.reshape(8, -1, 16).transpose(0, 2, 1)).reshape(128, -1).astype(np.int32)
def gcols(t, e):
    v = np.concatenate([t.reshape(8, 16, -1, 4), np.zeros((8, 16, 1, 4), BF)], axis=2)
    return np.ascontiguousarray(np.stack([v[g][:, e[g]] for g in range(8)])).reshape(128, -1)
def tile(rs):
    return np.stack(rs, axis=2).reshape(128, -1).astype(BF)
def pick(q, e):
    c = np.concatenate([q[0].reshape(128, -1, 4), np.zeros((128, 1, 4), np.uint8)], axis=1); s = np.concatenate([q[1], np.ones((16, 1), np.uint8)], axis=1)
    return (np.ascontiguousarray(c[:, e].reshape(128, -1)), np.ascontiguousarray(s[:, e]))
def join(*qs):
    return (np.concatenate([q[0] for q in qs], axis=1), np.concatenate([q[1] for q in qs], axis=1))
def put(q, e, v):
    c, s = q[0].reshape(128, -1, 4).copy(), q[1].copy(); c[:, e] = v[0].reshape(128, -1, 4); s[:, e] = v[1]
    return (c.reshape(128, -1), s)
def pk(c, s):
    return (np.ascontiguousarray(c), mx_ref.live(s))
def emit(q):
    return q[0], q[1]
def packed(v, rng):
    q = [mx_ref.quantize(np.ascontiguousarray(v[r])) for r in range(N)]
    return np.stack([a for a, b in q]), np.stack([mx_ref.plane(b, rng) for a, b in q])
def values_of_codes():
    e, c = np.zeros((128, 128, 4), np.float32), np.zeros((128, 2, 4), np.uint8)
    e[np.arange(128), np.arange(128), 0] = 1
    c[:127, :, 0] = np.arange(256).reshape(2, 128).T[:127]
    return mx_ref.matmul(mx_ref.quantize(e.reshape(128, 512).astype(BF)), (c.reshape(128, 8), np.full((16, 2), 127, np.uint8))).T.reshape(-1).astype(np.float64)
CODE_VALUE, SCALE_VALUE = values_of_codes(), 2.0 ** (np.arange(256) - 127.0)
def decode(q):
    return (CODE_VALUE[q[0]].reshape(16, 8, -1, 4) * SCALE_VALUE[q[1]][:, None, :, None] + 0.0).reshape(128, -1).astype(np.float32)
def f(rng, *shape):
    return mx_ref.flush((rng.standard_normal(shape, dtype=np.float32) * np.exp2(rng.integers(-2, 3, shape[:-1] + (1,)))).astype(BF))
def wide(rng, *shape, cols=0):
    v = rng.standard_normal(shape, dtype=np.float32) * np.exp2(rng.integers(-12, 13, shape)).astype(np.float32)
    if cols: v *= np.repeat(np.exp2(rng.integers(-cols, cols + 1, shape[:-2] + (1, shape[-1] // 4))) * (rng.random(shape[:-2] + (1, shape[-1] // 4)) > 0.0625), 4, axis=-1).astype(np.float32)
    return mx_ref.flush(v.astype(BF))
C, H = 448, 224
STEP = [1, 2, 3]
def numbers_of(rng):
    return {"x": np.array(f(rng, N, 128, 4 * C)), "u": np.array(f(rng, N, 128, 512)), "v": np.array(f(rng, N, 128, 512))}
def stored(m):
    return {"ml": np.stack([gtable(m[r]) for r in range(N)])}
def paired(e):
    m = np.zeros_like(e)
    np.put_along_axis(m, e, np.roll(e, H, axis=-1), axis=-1)
    return m
def pairings(rng):
    return paired(rng.permuted(np.tile(np.arange(C), (N, 8, 1)), axis=2))
def zigzag(rng, loop):
    s, t = rng.permutation(H), rng.permutation(H)
    a = np.concatenate([np.roll(t, -1), H + np.roll(s, -1)]).reshape(-1, 2)
    if not loop: a[H // 2 - 1, 1], a[-1, 0] = int(a[-1, 0]), int(a[H // 2 - 1, 1])
    b = np.concatenate([s, H + t]).reshape(-1, 2)
    return [paired(np.concatenate([k[:, 0], k[:, 1]])) for k in (a, b)]
def coil(rng):
    s = rng.permutation(H)
    k = np.concatenate([s, H + np.roll(s[:-1], -1), H + s[-1:]]).reshape(-1, 2)
    k[H // 2 - 1, 1], k[-1, 0] = int(k[-1, 0]), int(k[H // 2 - 1, 1])
    return paired(np.concatenate([k[:, 0], k[:, 1]]))
def layers(rng, still=[], pairs=False):
    w = np.array(f(rng, N, 128, 2048)).reshape(N, 8, 16, 4, 8, 16, 4)
    for i in still:
        w[:, :, i] = 0
        w[:, :, :, :, :, i] = 0
    if pairs:
        w[:, :, :, :, :, 8:] = 0
        for g in range(8):
            w[:, g, 8, 0, g, 8, 0] = -28.0
            for b in range(4): w[:, g, 10, b, g, 9, 0] = -2.0 ** (b - 5)
    return w
def weights(rng, w):
    c, s = packed(np.ascontiguousarray(w).reshape(N, 128, 2048), rng)
    return {"wc": c, "ws": s}
def setup_inputs(rng):
    return {**numbers_of(rng), **stored(pairings(rng)), **weights(rng, layers(rng))}
def setup_inputs_ties(rng):
    d = numbers_of(rng)
    o = rng.permutation(N)
    k = rng.integers(0, 4, (N, 8, C))
    k[o[0]] = 0
    k[o[1]] -= 4
    k[o[2]] = np.arange(C) < H
    kind = rng.permutation(8)
    m = np.zeros((N, 8, C), np.int64)
    for g in range(8):
        if 4 <= kind[g] < 7: k[:, g] = np.sort(k[:, g].reshape(N, 2, H), axis=1).reshape(N, C)
        for r in range(N):
            p, q = r ^ STEP[0], r ^ STEP[1]
            if kind[g] < 4 and r < p:
                a = zigzag(rng, kind[g] == 3)
                j = int(rng.integers(2))
                m[r, g], m[p, g] = a[j], a[1 - j]
            if 4 <= kind[g] < 6 and r < min(p, q, p ^ STEP[1]):
                m[r, g], m[q, g] = zigzag(rng, False)
                m[p, g] = m[p ^ STEP[1], g] = paired(np.arange(C))
            if kind[g] == 7: m[r, g] = paired(np.concatenate([rng.permutation(H), H + rng.permutation(H)]))
        if kind[g] == 6:
            m[:, g] = paired(np.arange(C))
            r = int(rng.integers(N))
            if STEP[0] ^ STEP[1] == STEP[2]: m[r, g] = coil(rng)
            else: m[r, g], m[r ^ STEP[2], g] = zigzag(rng, False)
    x = d["x"].reshape(N, 8, 16, C, 4)
    x[:, :, 0] = 0
    x[:, :, 0, :, 0] = k.astype(np.float32).astype(BF)
    a = np.exp2(rng.integers(-3, 4, (N, 8, 1)).astype(np.float32))
    x[:, :, 8:] = 0
    x[:, :, 8, :, 0] = (-1.125 * a).astype(BF)
    x[:, :, 10, :, 0] = (-0.0703125 * a).astype(BF)
    u = d["u"].reshape(N, 128, 128, 4)
    u[:, :, ::16] = 0
    for h in range(0, 128, 16): u[:, h, h, 0] = 1.0
    return {"x": x.reshape(N, 128, 4 * C), "u": u.reshape(N, 128, 512), "v": d["v"], **stored(twist(k, m)), **weights(rng, layers(rng, [0], True))}
def setup_inputs_near(rng):
    d = numbers_of(rng)
    x = d["x"].astype(np.float32).reshape(N, 8, 16, C, 4)
    x[:, :, 0] = 0
    x[:, :, 8:] = 0
    u = d["u"].reshape(N, 128, 128, 4)
    u[:, :, ::16] = 0
    w = layers(rng, [0, 8, 9, 10, 11, 12, 13, 14, 15])
    o = rng.permutation(N) % 4
    for r in range(N):
        c = rng.choice([-1.0, 1.0], (8, 1))
        s = rng.integers(0, 16, (8, C))
        digits = ((s[:, :, None] >> np.arange(4)) & 1) * np.exp2(np.arange(4) - 23.0)
        if o[r] < 2:
            x[r, :, 0, :, 0] = c
            x[r, :, 8] = digits
            x[r, :, 11, :, 0] = 2.0 ** -10
        elif o[r] == 2: x[r, :, 8] = digits * rng.choice([-1.0, 1.0], (8, C, 1))
        else:
            x[r, :, 8, :, 0] = np.where(s < 8, 1.25, 0.0) * 2.0 ** -30 * c
            x[r, :, 9, :, 0] = np.where(s < 8, 0.0, 1.125) * 2.0 ** -30 * c
            for g in rng.permutation(8)[:4]:
                e = rng.choice([-1.0, 1.0], C) * 2.0 ** -30
                x[r, g, 8, :, 0] = 1.25 * e
                x[r, g, 9, :, 0] = -1.125 * e
            for g in range(8):
                w[r, g, 8, 0, g, 12, 0] = 2.0 ** -8
                w[r, g, 8, 0, g, 14, 0] = 64.0
                w[r, g, 1, 0, g, 2, 0] = 256.0
        at = [0, C - 1, int(rng.integers(C)), int(rng.integers(C))]
        for g, j in zip(rng.permutation(8)[:4], at): x[r, g, 0, j, 0] = 2.0 ** 29 * rng.choice([-1.0, 1.0])
        k = 1.0 if o[r] == 0 else 2.0 ** -30
        for h in range(0, 128, 16):
            u[r, h, h, 0] = k if o[r] < 2 else 1.0
            if o[r] < 2: u[r, h + 11, h, 0] = k
            if o[r] < 3: u[r, h + 8, h] = k
            else:
                u[r, h + 8, h, 0] = k
                u[r, h + 9, h, 0] = 1.125 * k
                u[r, h + 12, h, 0] = k
    return {"x": x.reshape(N, 128, 4 * C).astype(BF), "u": u.reshape(N, 128, 512), "v": d["v"], **stored(pairings(rng)), **weights(rng, w)}
def setup_inputs_odd(rng):
    d = numbers_of(rng)
    x = (1.0 + (2 * rng.integers(0, 64, (N, 16, 8, C, 4)) + 1) * 2.0 ** -7) * np.exp2(-rng.integers(0, 7, (N, 16, 8, C, 4)).astype(np.float64)) * rng.choice([-1.0, 1.0], (N, 16, 8, C, 4))
    x[:, :, 0, :, 0] = 1.96875 * 2.0 ** 8 * rng.choice([-1.0, 1.0], (N, 16, C))
    u = d["u"].reshape(N, 16, 8, 128, 4)
    u[:, :, 0, ::16] = 0
    for r in range(N):
        for i, g in enumerate(rng.permutation(8)[:4]):
            x[r, 2 * g, 1, :, 0] = (8 + rng.integers(0, 2, C)) * 2.0 ** (i - 8)
            u[r, :, :, 16 * g] = 0
            u[r, 2 * g, 1, 16 * g, 0] = 1.0
    return {"x": x.astype(np.float32).reshape(N, 128, 4 * C).astype(BF), "u": u.reshape(N, 128, 512), "v": d["v"], **stored(pairings(rng)), **weights(rng, layers(rng, [0, 8]))}
def setup_inputs_ends(rng):
    d = numbers_of(rng)
    x = np.zeros((N, 8, 16, C, 4))
    u = d["u"].astype(np.float32).reshape(N, 128, 128, 4)
    v = d["v"].astype(np.float32)
    w = np.zeros((N, 128, 4, 128, 4), np.float32)
    m = pairings(rng)
    o, e = rng.permutation(N) % 4, rng.permutation(N) % 4
    i = np.arange(128)
    for r in range(N):
        h = rng.permutation(8)
        c = np.where(h < 2, 0.0, h % 2 * 2.0 - 1.0)[None, :, None]
        k = np.array([2.0, 4.0, -4.0])[rng.permutation(8) % 3]
        low = -(0.9 + 0.1 * rng.random((8, 16, C, 4))) * 2.0 ** 28
        if o[r] == 0: x[r] = low
        if o[r] == 1: x[r] = low * rng.choice([-1.0, 1.0], (C, 1))
        if o[r] < 2:
            u[r, :, ::16] = c * (0.9 + 0.1 * rng.random((128, 8, 4))) * 2.0 ** 30
            v[r] = rng.choice([-1.0, 1.0], (128, 512)) * (0.9 + 0.1 * rng.random((128, 512))) * 2.0 ** 30
        if o[r] == 2:
            x[r] = -(1.0 + 0.125 * rng.integers(0, 8, (8, 16, C, 4))) * 2.0 ** -30
            u[r, :, ::16] = c * (1.0 + 0.125 * rng.integers(0, 8, (128, 8, 4))) * 2.0 ** -30
            v[r] = rng.choice([-1.0, 1.0], (128, 512)) * (1.0 + 0.125 * rng.integers(0, 8, (128, 512))) * 2.0 ** -30
            k[:] = 32.0
        if o[r] == 3:
            x[r] = d["x"][r].astype(np.float32).reshape(8, 16, C, 4)[:, :, :1]
            u[r, :, ::16] *= np.abs(c).astype(np.float32)
        for b in range(4): w[r, i, b, i, b] = k[i // 16]
        if e[r] < 3: m[r] = [paired(np.arange(C)), np.arange(C) ^ 1, C - 1 - np.arange(C)][e[r]]
    return {"x": x.astype(np.float32).reshape(N, 128, 4 * C).astype(BF), "u": u.reshape(N, 128, 512).astype(BF), "v": v.astype(BF), **stored(m), **weights(rng, w.astype(BF))}
def setup_inputs_spread(rng):
    d = setup_inputs(rng)
    d["x"] = wide(rng, N, 128, 4 * C, cols=6)
    return d
def check_inputs(d):
    b = []
    for k in ("x", "u", "v"):
        a = np.abs(d[k].astype(np.float32))
        if not (np.isfinite(a).all() and ((a == 0) | (a >= 2.0 ** -30) & (a <= 2.0 ** 30)).all()): b.append("a value of " + k)
    none, least, most = [emit(mx_ref.quantize(np.full((128, 16), k, np.float32).astype(BF)))[1][0, 0] for k in (0.0, 2.0 ** -8, 2.0 ** 8)]
    for r in range(N):
        e = gentries(d["ml"][r]).astype(np.int64)
        if not ((e >= 0) & (e < C)).all(): b.append("an entry of ml")
        elif (e == np.arange(C)).any() or (np.take_along_axis(e, e, axis=1) != np.arange(C)).any(): b.append("ml: not a pairing")
        if ((d["wc"][r] == 0x7F) | (d["wc"][r] == 0xFF)).any(): b.append("wc: a code that is no number")
        s = mx_ref.live(d["ws"][r])
        if ((s != none) & ((s < least) | (s > most))).any(): b.append("ws: a scale out of range")
    return b
def twist(s, m):
    e = np.zeros(m.shape, np.int64) + np.arange(C)
    swap = H * (s[..., :H] > s[..., H:])
    e[..., :H] += swap
    e[..., H:] -= swap
    return np.take_along_axis(e, np.take_along_axis(m, e, axis=-1), axis=-1)
def glued(a, b):
    at = np.tile(np.arange(C), (8, 1))
    far = at >= H
    done = np.zeros((8, C), bool)
    for _ in range(H + 1):
        at = np.where(done, at, np.where(far, np.take_along_axis(b, at, axis=1), np.take_along_axis(a, at, axis=1)))
        done = done | ((at >= H) == far)
        at = np.where(done, at, np.where(far, at + H, at - H))
        far = far ^ ~done
        if done.all(): break
    return at
def plus(s, t):
    return (s.astype(np.float32) + t.astype(np.float32)).astype(BF)
def reference(x, u, v, ml, wc, ws):
    qu = [mx_ref.quantize(u[r]) for r in range(N)]
    lay = [pk(wc[r], ws[r]) for r in range(N)]
    now = [x[r] for r in range(N)]
    mate = [gentries(ml[r]).astype(np.int64) for r in range(N)]
    for step in STEP:
        turned, qa = [], []
        for r in range(N):
            s = mx_ref.matmul(qu[r], mx_ref.quantize(now[r]))[::16] + np.float32(0.0)
            turned.append(twist(s, mate[r]))
            qz = mx_ref.quantize(plus(now[r], gcols(now[r], turned[r])))
            qa.append(mx_ref.quantize(tile([mx_ref.matmul(pick(lay[r], np.arange(128 * b, 128 * b + 128)), qz) * np.float32(0.015625) for b in range(4)])))
        made = []
        for r in range(N):
            p = r ^ step
            mate[r] = glued(turned[r], turned[p])
            t = decode(join(pick(qa[r], np.arange(H)), pick(qa[p], np.arange(H, C)))).astype(BF)
            made.append(plus(now[r], gcols(t, mate[r])))
        now = made
    y, mo = np.zeros((N, 128, C), np.float32), np.zeros((N, 8, C), np.float32)
    oc, osc = np.zeros((N, 128, 4 * C), np.uint8), np.zeros((N, 16, C), np.uint8)
    for r in range(N):
        q = mx_ref.quantize(now[r])
        y[r] = mx_ref.matmul(mx_ref.quantize(v[r]), q)
        mo[r] = mate[r]
        oc[r], osc[r] = emit(q)
    return {"y": y, "mo": mo, "oc": oc, "osc": osc}

@@ -1,0 +1,353 @@
+from concourse.bass import DstId, RemoteDMATransfer
+from concourse.mybir import dt, AluOpType, ActivationFunctionType
+
+OP = AluOpType
+COPY = ActivationFunctionType.Copy
+C, H = 448, 224
+ROUNDS = [1, 2, 3]
+F16, BF, F32, I32, U16, U8, MX = "float16", "bfloat16", "float32", "int32", "uint16", "uint8", "float8_e4m3fn_x4"
+
+SCRATCH = {}
+
+
+def _sb(name, n, d):
+    SCRATCH[name] = ("sbuf", [128, n], d)
+
+
+for _r in range(4):
+    _sb("x%d" % _r, 4 * C, BF)
+for _b in range(4):
+    _sb("xp%d" % _b, C, BF)
+    _sb("bp%d" % _b, C, BF)
+for _n in ("zl", "zu", "al", "au"):
+    _sb(_n, 4 * H, BF)
+for _n, _w in (("uq", 128), ("uq2", 128), ("vq", 128), ("wq", 512), ("eq", 512), ("qx", C), ("qzl", H), ("qzu", H),
+               ("qal", H), ("qau", H)):
+    _sb(_n, _w, MX)
+    _sb(_n + "s", _w, U8)
+for _s in ROUNDS:
+    _sb("lq%d" % _s, H, MX)
+    _sb("lq%ds" % _s, H, U8)
+    _sb("lb%d" % _s, 28, U16)
+for _n, _w, _d in (("ut", 512, BF), ("vt", 512, BF), ("mli", 28, I32), ("ones", 2048, BF), ("et", 2048, BF),
+                   ("ii", 672, I32), ("mi", 672, I32), ("mask", 672, BF), ("rst", 672, BF), ("io", 672, F32),
+                   ("raw", C, F32), ("pi", 14, I32), ("pm", 14, I32), ("ci", 14, I32), ("idi", 14, I32),
+                   ("ui", 8, I32), ("up", 8, U16), ("mm", 42, U16), ("mf", 28, F32), ("sg", 28, F32), ("tt", 28, F32),
+                   ("mmf", 28, F32), ("sup", H, F32), ("sw", H, BF), ("ga", 672, F16), ("gb", 672, F16),
+                   ("sa", 672, F16), ("sm", C, F16), ("rr", 28, F32), ("qq", 28, F32), ("dd", 14, F32),
+                   ("ee", 14, F32), ("nn", 28, F32), ("n16", 28, U16), ("m16", 28, U16), ("la", 14, U16),
+                   ("lb", 14, U16), ("wa", C, F32), ("w0", 672, F32), ("w1", 672, F32), ("wu", C, F32),
+                   ("wf", C, F32), ("mrow", C, F32), ("yo", C, F32)):
+    _sb(_n, _w, _d)
+for _b in range(8):
+    SCRATCH["p%d" % _b] = ("psum", [128, 512], "float32")
+
+SEMAPHORES = ["v", "a", "t", "gp"] + ["d%d" % i for i in range(24)]
+for _s in ROUNDS:
+    for _k in ("b", "q", "s"):
+        SEMAPHORES += ["arr%s%d" % (_k, _s), "snt%s%d" % (_k, _s)]
+
+
+def rank_program(g, core, T, topo):
+    rank = T.rank_of(core)
+    if rank is None:
+        return
+    Q = {"v": g.vector, "a": g.scalar, "t": g.tensor, "g": g, "s": g.sync}
+    OWN = {"v": "v", "a": "a", "t": "t", "g": "gp"}
+    cnt, seen, snap, hist = {}, {q: {} for q in Q}, {}, {}
+    tick = [0]
+
+    def need(q, sem, val):
+        if seen[q].get(sem, 0) >= val:
+            return
+        Q[q].wait_ge(T.sem[sem], val)
+        for k, w in snap.get((sem, val), {}).items():
+            if seen[q].get(k, 0) < w:
+                seen[q][k] = w
+        seen[q][sem] = val
+
+    def meets(x, y):
+        (a, b, s), (c, d, t) = x, y
+        if a >= d or c >= b:
+            return False
+        return not (s == t and s > 1 and (a - c) % s)
+
+    def hazards(q, reads, writes):
+        tok = []
+        for kind, regs in ((0, reads), (1, writes)):
+            for n, a, b, s in regs:
+                ps = SCRATCH.get(n, ("",))[0] == "psum"
+                for reg, k, token, at, eng in hist.get(n, []):
+                    if ps and eng != q or (k or kind) and meets(reg, (a, b, s)):
+                        tok.append((at, token))
+        for at, (sem, val) in sorted(set(tok), reverse=True):
+            need(q, sem, val)
+
+    def note(q, reads, writes, token):
+        tick[0] += 1
+        for kind, regs in ((0, reads), (1, writes)):
+            for n, a, b, s in regs:
+                h = hist.setdefault(n, [])
+                if kind and s == 1:
+                    h[:] = [e for e in h if not (e[0][0] >= a and e[0][1] <= b)]
+                h.append(((a, b, s), kind, token, tick[0], q))
+
+    def op(q, writes, reads, call, sem=None, inc=1):
+        hazards(q, reads, writes)
+        sem = sem or OWN[q]
+        ins = call()
+        ins.then_inc(T.sem[sem], inc)
+        cnt[sem] = cnt.get(sem, 0) + inc
+        snap[(sem, cnt[sem])] = dict(seen[q])
+        note(q, reads, writes, (sem, cnt[sem]))
+
+    def R(n, a=0, b=None, s=1):
+        return (n, a, T[n].shape[1] if b is None else b, s)
+
+    def ap(r):
+        return T[r[0]][:, r[1]:r[2]] if r[3] == 1 else T[r[0]][:, r[1]:r[2]:r[3]]
+
+    def tt(out, x, y, o):
+        op("v", [out], [x, y], lambda: g.vector.tensor_tensor(ap(out), ap(x), ap(y), o))
+
+    def ts(out, x, s1, o1, s2=None, o2=None):
+        if o2 is None:
+            op("v", [out], [x], lambda: g.vector.tensor_scalar(ap(out), ap(x), s1, None, o1))
+        else:
+            op("v", [out], [x], lambda: g.vector.tensor_scalar(ap(out), ap(x), s1, s2, o1, o2))
+
+    def vcopy(out, x):
+        op("v", [out], [x], lambda: g.vector.tensor_copy(ap(out), ap(x)))
+
+    def fill(out, c):
+        op("v", [out], [], lambda: g.vector.memset(ap(out), c))
+
+    def pick_tt(out, win, off, y, o):
+        op("v", [out], [win, off, y], lambda: g.vector.tensor_tensor(ap(out), ap(win).indirect(ap(off)), ap(y), o))
+
+    def scan(out, x, n):
+        r = R("rst", 0, n)
+        op("v", [out], [x, r], lambda: g.vector.tensor_tensor_scan(ap(out), ap(r), ap(x), 0.0, OP.mult, OP.add))
+
+    def act(out, x, scale=1.0):
+        op("a", [out], [x], lambda: g.scalar.activation(ap(out), ap(x), COPY, scale=scale))
+
+    def act_pick(out, win, off):
+        op("a", [out], [win, off], lambda: g.scalar.activation(ap(out), ap(win).indirect(ap(off)), COPY))
+
+    def quant(q, x, a=0, b=None):
+        o, s = R(q, a, b), R(q + "s", a, b)
+        op("v", [o, s], [x], lambda: g.vector.quantize_mx(ap(o), ap(s), ap(x)))
+
+    def mm(bank, l, la, r, ra, rb):
+        o = R("p%d" % bank, 0, rb - ra)
+        ops = [R(l, la, la + 128), R(l + "s", la, la + 128), R(r, ra, rb), R(r + "s", ra, rb)]
+        op("t", [o], ops, lambda: g.tensor.matmul_mx(ap(o), ap(ops[0]), ap(ops[1]), ap(ops[2]), ap(ops[3]), True, True))
+
+    nd = [0]
+
+    def dma(q, writes, reads, out, in_):
+        sem = "d%d" % nd[0]
+        nd[0] += 1
+        op(q, writes, reads, lambda: Q[q].dma_start(out, in_), sem, 16)
+
+    def lanes(src, dst):
+        return topo.engines(src, dst)[:8]
+
+    def send(dst, land, src, k, s, codes):
+        e = lanes(core, dst)
+        rid, pid, _ = topo.addr(dst)
+        hazards("g", [src], [])
+        o, i = T[land][:, 0:src[2] - src[1]], ap(src)
+        if codes:
+            o, i = o.bitcast(dt.uint8), i.bitcast(dt.uint8)
+        g.remote_dma(out_ap=o, in_ap=i, remote_sem=T.sem["arr%s%d" % (k, s)], local_sem=T.sem["snt%s%d" % (k, s)],
+                     pid=pid, routing_id=rid, dma_engine_mask=sum(1 << j for j in e))
+        sem = "snt%s%d" % (k, s)
+        cnt[sem] = len(e)
+        note("g", [src], [], (sem, len(e)))
+
+    def arrives(land, k, s, src):
+        sem = "arr%s%d" % (k, s)
+        cnt[sem] = len(lanes(src, core))
+        note("g", [], [R(land)], (sem, cnt[sem]))
+
+    dma("a", [R("ut")], [], T.ut[:, :], T.u[:, :])
+    dma("s", [R("x0", 0, 4 * H)], [], T.x0[:, 0:4 * H], T.x[:, 0:4 * H])
+    dma("s", [R("x0", 4 * H, 4 * C)], [], T.x0[:, 4 * H:4 * C], T.x[:, 4 * H:4 * C])
+    dma("a", [R("mli")], [], T.mli[:, :], T.ml[:, :])
+    dma("s", [R("wq")], [], T.wq[:, :].bitcast(dt.uint8), T.wc[:, :])
+    dma("s", [R("wqs")], [], T.wqs[:, :], T.ws[:, :])
+    dma("s", [R("vt")], [], T.vt[:, :], T.v[:, :])
+
+    def iota(n, w, pattern, base, cm):
+        r = R(n, 0, w)
+        f = SCRATCH[n][2] == F32
+        op("g", [r], [], lambda: g.iota(ap(r), pattern, base, cm, allow_small_or_imprecise_dtypes=True) if f
+           else g.iota(ap(r), pattern, base, cm))
+
+    iota("ui", 8, [[16, 8]], 0, 0)
+    iota("ii", 672, [[0, 42], [1, 16]], 128, -1)
+    iota("pi", 14, [[0, 14]], 0, 1)
+    iota("ci", 14, [[16, 14]], 0, 0)
+    iota("io", 672, [[1, 672]], 0, 0)
+
+    fill(R("ones"), 1.0)
+    one = R("ones")
+    et = R("et")
+    op("g", [et], [one], lambda: g.affine_select(ap(et), ap(one), [[1, 4], [-1, 512]], OP.is_equal, 0.0, 0, 4))
+    vcopy(R("up"), R("ui"))
+    fill(R("rst"), 1.0)
+    fill(R("rst", 0, 672, 16), 0.0)
+    ts(R("mi"), R("ii"), 15, OP.bitwise_and)
+    ts(R("mask", 0, C), R("mi", 0, C), 0, OP.is_equal, 448.0, OP.mult)
+    ts(R("mask", C, 672), R("mi", C, 672), 0, OP.is_equal)
+    ts(R("pm"), R("pi"), 15, OP.bitwise_and)
+    tt(R("idi"), R("pm"), R("ci"), OP.add)
+    vcopy(R("mm", 28, 42), R("idi"))
+    mask1 = R("mask", C, 672)
+
+    quant("uq", R("ut"))
+    upk, uqc, uq2 = R("up"), R("uq"), R("uq2")
+    op("v", [uq2], [uqc, upk], lambda: g.vector.tensor_copy(ap(uq2).bitcast(dt.uint32), ap(uqc).bitcast(dt.uint32).indirect(ap(upk))))
+    us, us2 = R("uqs"), R("uq2s")
+    op("v", [us2], [us, upk], lambda: g.vector.tensor_copy(ap(us2), ap(us).indirect(ap(upk))))
+    for w in ("w0", "w1"):
+        act(R(w, H, 672), R("io", H, 672))
+    act(R("raw", 0, H), R("io", H, C))
+    act(R("raw", H, C), R("io", 0, H))
+    act(R("wa", H, C), R("io", C, 672))
+    act(R("wu", 0, H), R("io", 0, H))
+    act(R("wf", H, C), R("io", H, C))
+
+    vcopy(R("mf"), R("mli"))
+    mates = R("mf")
+
+    def prep(m):
+        ts(R("sg"), m, 224.0, OP.is_lt, 0.5, OP.subtract)
+        ts(R("tt"), m, 224.0, OP.is_ge, 224.0, OP.mult)
+        tt(R("mmf"), m, R("tt"), OP.subtract)
+        vcopy(R("mm", 0, 28), R("mmf"))
+
+    def planes(x, half):
+        for b in range(4):
+            act(R("xp%d" % b, half * H, half * H + H), R(x, half * 4 * H + b, half * 4 * H + 4 * H, 4))
+
+    def halfcols(x, half):
+        return R(x, half * 4 * H, half * 4 * H + 4 * H)
+
+    quant("qx", halfcols("x0", 0), 0, H)
+    mm(0, "uq2", 0, "qx", 0, H)
+    planes("x0", 0)
+    act(R("sup"), R("p0", 0, H))
+    quant("qx", halfcols("x0", 1), H, C)
+    mm(1, "uq2", 0, "qx", H, C)
+    prep(mates)
+    planes("x0", 1)
+
+    for s in ROUNDS:
+        last = s == ROUNDS[-1]
+        xs, xn = "x%d" % (s - 1), "x%d" % s
+        peer = T.cores[rank ^ s]
+        land_b, land_q = "lb%d" % s, "lq%d" % s
+        arrives(land_b, "b", s, peer)
+        arrives(land_q, "q", s, peer)
+        arrives(land_q + "s", "s", s, peer)
+
+        tt(R("sw"), R("sup"), R("p1", 0, H), OP.is_gt)
+        pick_tt(R("ga"), R("sw"), R("mm"), R("mask"), OP.mult)
+        scan(R("sa"), R("ga"), 672)
+        tt(R("rr"), R("sa", 15, C, 16), R("sg"), OP.mult)
+        tt(R("qq"), R("rr"), mates, OP.add)
+        tt(R("dd"), R("qq", 14, 28), R("qq", 0, 14), OP.subtract)
+        tt(R("ee"), R("dd"), R("sa", C + 15, 672, 16), OP.mult)
+        tt(R("nn", 0, 14), R("qq", 0, 14), R("ee"), OP.add)
+        tt(R("nn", 14, 28), R("qq", 14, 28), R("ee"), OP.subtract)
+        vcopy(R("n16"), R("nn"))
+        send(peer, land_b, R("n16"), "b", s, False)
+        n_up, n_lo = R("n16", 0, 14), R("n16", 14, 28)
+        b_up, b_lo = R(land_b, 0, 14), R(land_b, 14, 28)
+
+        act_pick(R("wa", 0, H), R("raw"), n_lo)
+        for b in range(4):
+            pick_tt(R("zl", b, 4 * H, 4), R("xp%d" % b), n_lo, R(xs, 4 * H + b, 4 * C, 4), OP.add)
+        quant("qzl", R("zl"))
+        for b in range(4):
+            mm(2 + b, "wq", 128 * b, "qzl", 0, H)
+            act(R("al", b, 4 * H, 4), R("p%d" % (2 + b), 0, H), 0.015625)
+        for b in range(4):
+            pick_tt(R("zu", b, 4 * H, 4), R("xp%d" % b), n_up, R(xs, b, 4 * H, 4), OP.add)
+        quant("qzu", R("zu"))
+        quant("qal", R("al"))
+        send(peer, land_q, R("qal"), "q", s, True)
+        send(peer, land_q + "s", R("qals"), "s", s, False)
+        for b in range(4):
+            k = (6, 7, 2, 3)[b]
+            mm(k, "wq", 128 * b, "qzu", 0, H)
+            act(R("au", b, 4 * H, 4), R("p%d" % k, 0, H), 0.015625)
+        if s == 1:
+            quant("eq", R("et"))
+            quant("vq", R("vt"))
+
+        gbuf = ("ga", "gb")
+        lists = ("la", "lb")
+        win, lst = R("wa"), b_up
+        for k in range(7):
+            gk, lk, wk = R(gbuf[k % 2], 0, H), R(lists[k % 2]), "w%d" % (k % 2)
+            pick_tt(gk, win, lst, mask1, OP.mult)
+            act_pick(R(wk, 0, H), win, lst)
+            scan(R("sa", 0, H), gk, H)
+            vcopy(lk, R("sa", 15, H, 16))
+            if k == 0:
+                quant("qau", R("au"))
+                for b in range(4):
+                    mm(4 + b, "eq", 128 * b, "qau", 0, H)
+            if 0 < k < 5:
+                act(R("bp%d" % (k - 1), 0, H), R("p%d" % (3 + k), 0, H))
+            win, lst = R(wk), lk
+        for b in range(4):
+            mm(2 + b, "eq", 128 * b, land_q, 0, H)
+        w_up = R("wu", H, C)
+        op("v", [w_up], [win, lst], lambda: g.vector.tensor_scalar(ap(w_up), ap(win).indirect(ap(lst)), 224.0, None, OP.subtract))
+        pick_tt(R("ga", 0, H), R("wu"), n_up, mask1, OP.mult)
+        act_pick(R("wf", 0, H), R("wu"), n_lo)
+        for b in range(4):
+            act(R("bp%d" % b, H, C), R("p%d" % (2 + b), 0, H))
+        scan(R("sm", 0, H), R("ga", 0, H), H)
+        vcopy(R("m16", 0, 14), R("sm", 15, H, 16))
+        pick_tt(R("gb", 0, H), R("wf"), b_lo, mask1, OP.mult)
+        scan(R("sm", H, C), R("gb", 0, H), H)
+        vcopy(R("m16", 14, 28), R("sm", H + 15, C, 16))
+        mates = R("sm", 15, C, 16)
+
+        for half in (0, 1):
+            for b in range(4):
+                lo = half * 4 * H + b
+                hi = half * 4 * H + 4 * H
+                pick_tt(R(xn, lo, hi, 4), R("bp%d" % b), R("m16", 14 * half, 14 * half + 14), R(xs, lo, hi, 4), OP.add)
+            quant("qx", halfcols(xn, half), half * H, half * H + H)
+            if not last:
+                mm(half, "uq2", 0, "qx", half * H, half * H + H)
+                if half == 1:
+                    prep(mates)
+                planes(xn, half)
+                if half == 0:
+                    act(R("sup"), R("p0", 0, H))
+            else:
+                c0, c1 = half * H, half * H + H
+                mm(half, "vq", 0, "qx", c0, c1)
+                dma("s", [], [R("qx", c0, c1)], T.oc[:, 4 * c0:4 * c1], T.qx[:, c0:c1].bitcast(dt.uint8))
+                if half == 0:
+                    act_pick(R("mrow", 0, H), R("wu"), n_up)
+                    act_pick(R("mrow", H, C), R("wf"), b_lo)
+                    act(R("yo", 0, H), R("p0", 0, H))
+                    dma("s", [], [R("mrow")], T.mo[:, :], T.mrow[0:128:16, :])
+                    dma("s", [], [R("yo", 0, H)], T.y[:, 0:H], T.yo[:, 0:H])
+                else:
+                    for k in range(4):
+                        dma("s" if k < 2 else "a", [], [R("qxs")], T.osc[4 * k:4 * k + 4, :], T.qxs[32 * k:32 * k + 4, :])
+                    vcopy(R("yo", H, C), R("p1", 0, H))
+                    dma("a", [], [R("yo", H, C)], T.y[:, H:C], T.yo[:, H:C])
+
+    for sem in sorted(cnt):
+        need("g", sem, cnt[sem])

@@ -1,4 +1,3 @@
-from concourse.bass import DstId, RemoteDMATransfer
 from concourse.mybir import dt, AluOpType, ActivationFunctionType
 
 OP = AluOpType
@@ -29,14 +28,16 @@ for _s in ROUNDS:
     _sb("lq%d" % _s, H, MX)
     _sb("lq%ds" % _s, H, U8)
     _sb("lb%d" % _s, 28, U16)
-for _n, _w, _d in (("ut", 512, BF), ("vt", 512, BF), ("mli", 28, I32), ("ones", 2048, BF), ("et", 2048, BF),
-                   ("ii", 672, I32), ("mi", 672, I32), ("mask", 672, BF), ("rst", 672, BF), ("io", 672, F32),
-                   ("raw", C, F32), ("pi", 14, I32), ("pm", 14, I32), ("ci", 14, I32), ("idi", 14, I32),
-                   ("ui", 8, I32), ("up", 8, U16), ("mm", 42, U16), ("mf", 28, F32), ("sg", 28, F32), ("tt", 28, F32),
-                   ("mmf", 28, F32), ("sup", H, F32), ("sw", H, BF), ("ga", 672, F16), ("gb", 672, F16),
-                   ("sa", 672, F16), ("sm", C, F16), ("rr", 28, F32), ("qq", 28, F32), ("dd", 14, F32),
-                   ("ee", 14, F32), ("nn", 28, F32), ("n16", 28, U16), ("m16", 28, U16), ("la", 14, U16),
-                   ("lb", 14, U16), ("wa", C, F32), ("w0", 672, F32), ("w1", 672, F32), ("wu", C, F32),
+for _n, _w, _d in (("ut", 512, BF), ("vt", 512, BF), ("mli", 28, I32), ("ones", 512, BF), ("et", 2048, BF),
+                   ("pi", 42, I32), ("pm", 42, I32), ("pmu", 42, U16), ("pf", 1, F32), ("pf1", 1, F32), ("off", 1, F32),
+                   ("fi", 16, F32), ("ka", 16, F32), ("kb", 16, F32), ("k16", 16, BF), ("m1", 16, BF),
+                   ("keep", H, BF), ("mask", H, BF), ("rst", H, BF), ("io", 672, F32), ("raw", C, F32),
+                   ("ui", 8, I32), ("up", 8, U16), ("mm", 28, U16), ("mf", 28, F32), ("sg", 28, F32), ("tt", 28, F32),
+                   ("os0", 28, F32), ("mf2", 28, F32), ("af", 14, F32),
+                   ("mmf", 28, F32), ("sup", H, F32), ("sw", H, BF), ("bu", H, BF), ("bl", H, BF), ("sc", 672, BF),
+                   ("ga", H, F16), ("gb", H, F16), ("sa", H, F16), ("sm", C, F16), ("rr", 28, F32), ("qq", 28, F32),
+                   ("dd", 14, F32), ("ee", 14, F32), ("nn", 28, F32), ("n16", 28, U16), ("m16", 28, U16),
+                   ("la", 14, U16), ("lb", 14, U16), ("wa", C, F32), ("w0", 672, F32), ("w1", 672, F32), ("wu", C, F32),
                    ("wf", C, F32), ("mrow", C, F32), ("yo", C, F32)):
     _sb(_n, _w, _d)
 for _b in range(8):
@@ -116,6 +117,12 @@ def rank_program(g, core, T, topo):
         else:
             op("v", [out], [x], lambda: g.vector.tensor_scalar(ap(out), ap(x), s1, s2, o1, o2))
 
+    def tsp(out, x, sc, o1, s2=None, o2=None):
+        if o2 is None:
+            op("v", [out], [x, sc], lambda: g.vector.tensor_scalar(ap(out), ap(x), ap(sc), None, o1))
+        else:
+            op("v", [out], [x, sc], lambda: g.vector.tensor_scalar(ap(out), ap(x), ap(sc), s2, o1, o2))
+
     def vcopy(out, x):
         op("v", [out], [x], lambda: g.vector.tensor_copy(ap(out), ap(x)))
 
@@ -125,9 +132,13 @@ def rank_program(g, core, T, topo):
     def pick_tt(out, win, off, y, o):
         op("v", [out], [win, off, y], lambda: g.vector.tensor_tensor(ap(out), ap(win).indirect(ap(off)), ap(y), o))
 
-    def scan(out, x, n):
-        r = R("rst", 0, n)
+    def scan(out, x):
+        r = R("rst")
         op("v", [out], [x, r], lambda: g.vector.tensor_tensor_scan(ap(out), ap(r), ap(x), 0.0, OP.mult, OP.add))
+
+    def held(out, x):
+        r = R("keep")
+        op("v", [out], [x, r], lambda: g.vector.tensor_tensor_scan(ap(out), ap(r), ap(x), 0.0, OP.add, OP.max))
 
     def act(out, x, scale=1.0):
         op("a", [out], [x], lambda: g.scalar.activation(ap(out), ap(x), COPY, scale=scale))
@@ -186,30 +197,36 @@ def rank_program(g, core, T, topo):
         op("g", [r], [], lambda: g.iota(ap(r), pattern, base, cm, allow_small_or_imprecise_dtypes=True) if f
            else g.iota(ap(r), pattern, base, cm))
 
+    iota("pi", 42, [[0, 42]], 0, 1)
+    iota("fi", 16, [[1, 16]], 0, 0)
     iota("ui", 8, [[16, 8]], 0, 0)
-    iota("ii", 672, [[0, 42], [1, 16]], 128, -1)
-    iota("pi", 14, [[0, 14]], 0, 1)
-    iota("ci", 14, [[16, 14]], 0, 0)
     iota("io", 672, [[1, 672]], 0, 0)
-
-    fill(R("ones"), 1.0)
-    one = R("ones")
-    et = R("et")
-    op("g", [et], [one], lambda: g.affine_select(ap(et), ap(one), [[1, 4], [-1, 512]], OP.is_equal, 0.0, 0, 4))
-    vcopy(R("up"), R("ui"))
-    fill(R("rst"), 1.0)
-    fill(R("rst", 0, 672, 16), 0.0)
-    ts(R("mi"), R("ii"), 15, OP.bitwise_and)
-    ts(R("mask", 0, C), R("mi", 0, C), 0, OP.is_equal, 448.0, OP.mult)
-    ts(R("mask", C, 672), R("mi", C, 672), 0, OP.is_equal)
     ts(R("pm"), R("pi"), 15, OP.bitwise_and)
-    tt(R("idi"), R("pm"), R("ci"), OP.add)
-    vcopy(R("mm", 28, 42), R("idi"))
-    mask1 = R("mask", C, 672)
+    fill(R("ones"), 1.0)
+    vcopy(R("pmu"), R("pm"))
+    vcopy(R("pf"), R("pm", 0, 1))
+    vcopy(R("up"), R("ui"))
+    one = R("ones")
+    for b in range(4):
+        e = R("et", 512 * b, 512 * b + 512)
+        op("g", [e], [one], lambda: g.affine_select(ap(e), ap(one), [[-1, 512]], OP.is_equal, 0.0, b, 4))
+    pf, pf1, off = R("pf"), R("pf1"), R("off")
+    ts(pf1, pf, 1.0, OP.add)
+    ts(off, pf, 15.0, OP.is_lt, 2.0, OP.mult)
+    tsp(R("ka"), R("fi"), pf, OP.is_le, -8.0, OP.mult)
+    tsp(R("m1"), R("fi"), pf, OP.is_equal)
+    tsp(R("kb"), R("fi"), pf1, OP.is_equal, 2.0, OP.mult)
+    fill(R("rst"), 1.0)
+    tt(R("k16"), R("ka"), R("kb"), OP.add)
+    fill(R("rst", 0, H, 16), 0.0)
+    act_pick(R("mask"), R("m1"), R("pmu", 0, 14))
+    act_pick(R("keep"), R("k16"), R("pmu", 0, 14))
+    mask1 = R("mask")
 
     quant("uq", R("ut"))
     upk, uqc, uq2 = R("up"), R("uq"), R("uq2")
-    op("v", [uq2], [uqc, upk], lambda: g.vector.tensor_copy(ap(uq2).bitcast(dt.uint32), ap(uqc).bitcast(dt.uint32).indirect(ap(upk))))
+    op("v", [uq2], [uqc, upk],
+       lambda: g.vector.tensor_copy(ap(uq2).bitcast(dt.uint32), ap(uqc).bitcast(dt.uint32).indirect(ap(upk))))
     us, us2 = R("uqs"), R("uq2s")
     op("v", [us2], [us, upk], lambda: g.vector.tensor_copy(ap(us2), ap(us).indirect(ap(upk))))
     for w in ("w0", "w1"):
@@ -220,30 +237,30 @@ def rank_program(g, core, T, topo):
     act(R("wu", 0, H), R("io", 0, H))
     act(R("wf", H, C), R("io", H, C))
 
-    vcopy(R("mf"), R("mli"))
-    mates = R("mf")
-
     def prep(m):
-        ts(R("sg"), m, 224.0, OP.is_lt, 0.5, OP.subtract)
         ts(R("tt"), m, 224.0, OP.is_ge, 224.0, OP.mult)
+        ts(R("sg"), R("tt"), -2.0, OP.mult, 224.0, OP.add)
         tt(R("mmf"), m, R("tt"), OP.subtract)
-        vcopy(R("mm", 0, 28), R("mmf"))
+        tsp(R("os0"), R("sg"), off, OP.mult)
+        vcopy(R("mm"), R("mmf"))
+        tt(R("mf2"), m, R("os0"), OP.subtract)
 
-    def planes(x, half):
-        for b in range(4):
-            act(R("xp%d" % b, half * H, half * H + H), R(x, half * 4 * H + b, half * 4 * H + 4 * H, 4))
+    def plane(x, half, b):
+        act(R("xp%d" % b, half * H, half * H + H), R(x, half * 4 * H + b, half * 4 * H + 4 * H, 4))
 
     def halfcols(x, half):
         return R(x, half * 4 * H, half * 4 * H + 4 * H)
 
+    vcopy(R("mf"), R("mli"))
     quant("qx", halfcols("x0", 0), 0, H)
     mm(0, "uq2", 0, "qx", 0, H)
-    planes("x0", 0)
+    plane("x0", 0, 0)
+    plane("x0", 0, 1)
     act(R("sup"), R("p0", 0, H))
     quant("qx", halfcols("x0", 1), H, C)
     mm(1, "uq2", 0, "qx", H, C)
-    prep(mates)
-    planes("x0", 1)
+    prep(R("mf"))
+    todo = [(0, 2), (0, 3)]
 
     for s in ROUNDS:
         last = s == ROUNDS[-1]
@@ -255,12 +272,20 @@ def rank_program(g, core, T, topo):
         arrives(land_q + "s", "s", s, peer)
 
         tt(R("sw"), R("sup"), R("p1", 0, H), OP.is_gt)
-        pick_tt(R("ga"), R("sw"), R("mm"), R("mask"), OP.mult)
-        scan(R("sa"), R("ga"), 672)
-        tt(R("rr"), R("sa", 15, C, 16), R("sg"), OP.mult)
-        tt(R("qq"), R("rr"), mates, OP.add)
+        bu, sw, up = R("bu"), R("sw"), R("mm", 0, 14)
+        op("v", [bu], [sw, up], lambda: g.vector.tensor_copy(ap(bu), ap(sw).indirect(ap(up))))
+        act_pick(R("bl"), sw, R("mm", 14, 28))
+        for half, b in todo + [(1, b) for b in range(4)]:
+            plane(xs, half, b)
+        todo = []
+        held(R("sc", C, 672), sw)
+        held(R("sc", 0, H), bu)
+        held(R("sc", H, C), R("bl"))
+        tsp(R("af"), R("sc", C + 15, 672, 16), off, OP.subtract)
+        tt(R("rr"), R("sc", 15, C, 16), R("sg"), OP.mult)
+        tt(R("qq"), R("rr"), R("mf2"), OP.add)
         tt(R("dd"), R("qq", 14, 28), R("qq", 0, 14), OP.subtract)
-        tt(R("ee"), R("dd"), R("sa", C + 15, 672, 16), OP.mult)
+        tt(R("ee"), R("dd"), R("af"), OP.mult)
         tt(R("nn", 0, 14), R("qq", 0, 14), R("ee"), OP.add)
         tt(R("nn", 14, 28), R("qq", 14, 28), R("ee"), OP.subtract)
         vcopy(R("n16"), R("nn"))
@@ -269,14 +294,20 @@ def rank_program(g, core, T, topo):
         b_up, b_lo = R(land_b, 0, 14), R(land_b, 14, 28)
 
         act_pick(R("wa", 0, H), R("raw"), n_lo)
+
+        def z(half, b):
+            pick_tt(R(("zu", "zl")[half], b, 4 * H, 4), R("xp%d" % b), (n_up, n_lo)[half],
+                    R(xs, half * 4 * H + b, half * 4 * H + 4 * H, 4), OP.add)
+
         for b in range(4):
-            pick_tt(R("zl", b, 4 * H, 4), R("xp%d" % b), n_lo, R(xs, 4 * H + b, 4 * C, 4), OP.add)
+            z(1, b)
+        z(0, 0)
         quant("qzl", R("zl"))
         for b in range(4):
             mm(2 + b, "wq", 128 * b, "qzl", 0, H)
             act(R("al", b, 4 * H, 4), R("p%d" % (2 + b), 0, H), 0.015625)
-        for b in range(4):
-            pick_tt(R("zu", b, 4 * H, 4), R("xp%d" % b), n_up, R(xs, b, 4 * H, 4), OP.add)
+        for b in range(1, 4):
+            z(0, b)
         quant("qzu", R("zu"))
         quant("qal", R("al"))
         send(peer, land_q, R("qal"), "q", s, True)
@@ -293,48 +324,57 @@ def rank_program(g, core, T, topo):
         lists = ("la", "lb")
         win, lst = R("wa"), b_up
         for k in range(7):
-            gk, lk, wk = R(gbuf[k % 2], 0, H), R(lists[k % 2]), "w%d" % (k % 2)
+            gk, lk, wk = R(gbuf[k % 2]), R(lists[k % 2]), "w%d" % (k % 2)
             pick_tt(gk, win, lst, mask1, OP.mult)
             act_pick(R(wk, 0, H), win, lst)
-            scan(R("sa", 0, H), gk, H)
-            vcopy(lk, R("sa", 15, H, 16))
-            if k == 0:
+            if k == 1:
                 quant("qau", R("au"))
                 for b in range(4):
                     mm(4 + b, "eq", 128 * b, "qau", 0, H)
-            if 0 < k < 5:
-                act(R("bp%d" % (k - 1), 0, H), R("p%d" % (3 + k), 0, H))
+            scan(R("sa"), gk)
+            vcopy(lk, R("sa", 15, H, 16))
+            if 1 < k < 6:
+                act(R("bp%d" % (k - 2), 0, H), R("p%d" % (2 + k), 0, H))
             win, lst = R(wk), lk
         for b in range(4):
             mm(2 + b, "eq", 128 * b, land_q, 0, H)
         w_up = R("wu", H, C)
-        op("v", [w_up], [win, lst], lambda: g.vector.tensor_scalar(ap(w_up), ap(win).indirect(ap(lst)), 224.0, None, OP.subtract))
-        pick_tt(R("ga", 0, H), R("wu"), n_up, mask1, OP.mult)
+        op("v", [w_up], [win, lst],
+           lambda: g.vector.tensor_scalar(ap(w_up), ap(win).indirect(ap(lst)), 224.0, None, OP.subtract))
+        pick_tt(R("ga"), R("wu"), n_up, mask1, OP.mult)
         act_pick(R("wf", 0, H), R("wu"), n_lo)
         for b in range(4):
             act(R("bp%d" % b, H, C), R("p%d" % (2 + b), 0, H))
-        scan(R("sm", 0, H), R("ga", 0, H), H)
-        vcopy(R("m16", 0, 14), R("sm", 15, H, 16))
-        pick_tt(R("gb", 0, H), R("wf"), b_lo, mask1, OP.mult)
-        scan(R("sm", H, C), R("gb", 0, H), H)
-        vcopy(R("m16", 14, 28), R("sm", H + 15, C, 16))
-        mates = R("sm", 15, C, 16)
 
+        def new(half, b):
+            lo, hi = half * 4 * H + b, half * 4 * H + 4 * H
+            pick_tt(R(xn, lo, hi, 4), R("bp%d" % b), R("m16", 14 * half, 14 * half + 14), R(xs, lo, hi, 4), OP.add)
+
+        scan(R("sm", 0, H), R("ga"))
+        vcopy(R("m16", 0, 14), R("sm", 15, H, 16))
+        pick_tt(R("gb"), R("wf"), b_lo, mask1, OP.mult)
+        new(0, 0)
+        scan(R("sm", H, C), R("gb"))
+        new(0, 1)
+        vcopy(R("m16", 14, 28), R("sm", H + 15, C, 16))
+        new(0, 2)
+        new(0, 3)
+        new(1, 0)
         for half in (0, 1):
-            for b in range(4):
-                lo = half * 4 * H + b
-                hi = half * 4 * H + 4 * H
-                pick_tt(R(xn, lo, hi, 4), R("bp%d" % b), R("m16", 14 * half, 14 * half + 14), R(xs, lo, hi, 4), OP.add)
-            quant("qx", halfcols(xn, half), half * H, half * H + H)
+            if half == 1:
+                for b in range(1, 4):
+                    new(1, b)
+            c0, c1 = half * H, half * H + H
+            quant("qx", halfcols(xn, half), c0, c1)
             if not last:
-                mm(half, "uq2", 0, "qx", half * H, half * H + H)
+                mm(half, "uq2", 0, "qx", c0, c1)
                 if half == 1:
-                    prep(mates)
-                planes(xn, half)
-                if half == 0:
+                    prep(R("sm", 15, C, 16))
+                else:
+                    for b in range(4):
+                        plane(xn, 0, b)
                     act(R("sup"), R("p0", 0, H))
             else:
-                c0, c1 = half * H, half * H + H
                 mm(half, "vq", 0, "qx", c0, c1)
                 dma("s", [], [R("qx", c0, c1)], T.oc[:, 4 * c0:4 * c1], T.qx[:, c0:c1].bitcast(dt.uint8))
                 if half == 0:
@@ -344,10 +384,10 @@ def rank_program(g, core, T, topo):
                     dma("s", [], [R("mrow")], T.mo[:, :], T.mrow[0:128:16, :])
                     dma("s", [], [R("yo", 0, H)], T.y[:, 0:H], T.yo[:, 0:H])
                 else:
-                    for k in range(4):
-                        dma("s" if k < 2 else "a", [], [R("qxs")], T.osc[4 * k:4 * k + 4, :], T.qxs[32 * k:32 * k + 4, :])
                     vcopy(R("yo", H, C), R("p1", 0, H))
                     dma("a", [], [R("yo", H, C)], T.y[:, H:C], T.yo[:, H:C])
+                    for k in range(4):
+                        dma("s" if k < 2 else "a", [], [R("qxs")], T.osc[4 * k:4 * k + 4, :], T.qxs[32 * k:32 * k + 4, :])
 
     for sem in sorted(cnt):
         need("g", sem, cnt[sem])

from concourse.mybir import dt, AluOpType, ActivationFunctionType

OP = AluOpType
COPY = ActivationFunctionType.Copy
C, H = 448, 224
ROUNDS = [1, 2, 3]
F16, BF, F32, I32, U16, U8, MX = "float16", "bfloat16", "float32", "int32", "uint16", "uint8", "float8_e4m3fn_x4"

SCRATCH = {}


def _sb(name, n, d):
    SCRATCH[name] = ("sbuf", [128, n], d)


for _r in range(4):
    _sb("x%d" % _r, 4 * C, BF)
for _b in range(4):
    _sb("xp%d" % _b, C, BF)
    _sb("bp%d" % _b, C, BF)
for _n in ("zl", "zu", "al", "au"):
    _sb(_n, 4 * H, BF)
for _n, _w in (("uq", 128), ("uq2", 128), ("vq", 128), ("wq", 512), ("eq", 512), ("qx", C), ("qzl", H), ("qzu", H),
               ("qal", H), ("qau", H)):
    _sb(_n, _w, MX)
    _sb(_n + "s", _w, U8)
for _s in ROUNDS:
    _sb("lq%d" % _s, H, MX)
    _sb("lq%ds" % _s, H, U8)
    _sb("lb%d" % _s, 28, U16)
for _n, _w, _d in (("ut", 512, BF), ("vt", 512, BF), ("mli", 28, I32), ("ones", 512, BF), ("et", 2048, BF),
                   ("pi", 42, I32), ("pm", 42, I32), ("pmu", 42, U16), ("pf", 1, F32), ("pf1", 1, F32), ("off", 1, F32),
                   ("fi", 16, F32), ("ka", 16, F32), ("kb", 16, F32), ("k16", 16, BF), ("m1", 16, BF),
                   ("keep", H, BF), ("mask", H, BF), ("rst", H, BF), ("io", 672, F32), ("raw", C, F32),
                   ("ui", 8, I32), ("up", 8, U16), ("mm", 28, U16), ("mf", 28, F32), ("sg", 28, F32), ("tt", 28, F32),
                   ("os0", 28, F32), ("mf2", 28, F32), ("af", 14, F32),
                   ("mmf", 28, F32), ("sup", H, F32), ("sw", H, BF), ("bu", H, BF), ("bl", H, BF), ("sc", 672, BF),
                   ("ga", H, F16), ("gb", H, F16), ("sa", H, F16), ("sm", C, F16), ("rr", 28, F32), ("qq", 28, F32),
                   ("dd", 14, F32), ("ee", 14, F32), ("nn", 28, F32), ("n16", 28, U16), ("m16", 28, U16),
                   ("la", 14, U16), ("lb", 14, U16), ("wa", C, F32), ("w0", 672, F32), ("w1", 672, F32), ("wu", C, F32),
                   ("wf", C, F32), ("mrow", C, F32), ("yo", C, F32)):
    _sb(_n, _w, _d)
for _b in range(8):
    SCRATCH["p%d" % _b] = ("psum", [128, 512], "float32")

SEMAPHORES = ["v", "a", "t", "gp"] + ["d%d" % i for i in range(24)]
for _s in ROUNDS:
    for _k in ("b", "q", "s"):
        SEMAPHORES += ["arr%s%d" % (_k, _s), "snt%s%d" % (_k, _s)]


def rank_program(g, core, T, topo):
    rank = T.rank_of(core)
    if rank is None:
        return
    Q = {"v": g.vector, "a": g.scalar, "t": g.tensor, "g": g, "s": g.sync}
    OWN = {"v": "v", "a": "a", "t": "t", "g": "gp"}
    cnt, seen, snap, hist = {}, {q: {} for q in Q}, {}, {}
    tick = [0]

    def need(q, sem, val):
        if seen[q].get(sem, 0) >= val:
            return
        Q[q].wait_ge(T.sem[sem], val)
        for k, w in snap.get((sem, val), {}).items():
            if seen[q].get(k, 0) < w:
                seen[q][k] = w
        seen[q][sem] = val

    def meets(x, y):
        (a, b, s), (c, d, t) = x, y
        if a >= d or c >= b:
            return False
        return not (s == t and s > 1 and (a - c) % s)

    def hazards(q, reads, writes):
        tok = []
        for kind, regs in ((0, reads), (1, writes)):
            for n, a, b, s in regs:
                ps = SCRATCH.get(n, ("",))[0] == "psum"
                for reg, k, token, at, eng in hist.get(n, []):
                    if ps and eng != q or (k or kind) and meets(reg, (a, b, s)):
                        tok.append((at, token))
        for at, (sem, val) in sorted(set(tok), reverse=True):
            need(q, sem, val)

    def note(q, reads, writes, token):
        tick[0] += 1
        for kind, regs in ((0, reads), (1, writes)):
            for n, a, b, s in regs:
                h = hist.setdefault(n, [])
                if kind and s == 1:
                    h[:] = [e for e in h if not (e[0][0] >= a and e[0][1] <= b)]
                h.append(((a, b, s), kind, token, tick[0], q))

    def op(q, writes, reads, call, sem=None, inc=1):
        hazards(q, reads, writes)
        sem = sem or OWN[q]
        ins = call()
        ins.then_inc(T.sem[sem], inc)
        cnt[sem] = cnt.get(sem, 0) + inc
        snap[(sem, cnt[sem])] = dict(seen[q])
        note(q, reads, writes, (sem, cnt[sem]))

    def R(n, a=0, b=None, s=1):
        return (n, a, T[n].shape[1] if b is None else b, s)

    def ap(r):
        return T[r[0]][:, r[1]:r[2]] if r[3] == 1 else T[r[0]][:, r[1]:r[2]:r[3]]

    def tt(out, x, y, o):
        op("v", [out], [x, y], lambda: g.vector.tensor_tensor(ap(out), ap(x), ap(y), o))

    def ts(out, x, s1, o1, s2=None, o2=None):
        if o2 is None:
            op("v", [out], [x], lambda: g.vector.tensor_scalar(ap(out), ap(x), s1, None, o1))
        else:
            op("v", [out], [x], lambda: g.vector.tensor_scalar(ap(out), ap(x), s1, s2, o1, o2))

    def tsp(out, x, sc, o1, s2=None, o2=None):
        if o2 is None:
            op("v", [out], [x, sc], lambda: g.vector.tensor_scalar(ap(out), ap(x), ap(sc), None, o1))
        else:
            op("v", [out], [x, sc], lambda: g.vector.tensor_scalar(ap(out), ap(x), ap(sc), s2, o1, o2))

    def vcopy(out, x):
        op("v", [out], [x], lambda: g.vector.tensor_copy(ap(out), ap(x)))

    def fill(out, c):
        op("v", [out], [], lambda: g.vector.memset(ap(out), c))

    def pick_tt(out, win, off, y, o):
        op("v", [out], [win, off, y], lambda: g.vector.tensor_tensor(ap(out), ap(win).indirect(ap(off)), ap(y), o))

    def scan(out, x):
        r = R("rst")
        op("v", [out], [x, r], lambda: g.vector.tensor_tensor_scan(ap(out), ap(r), ap(x), 0.0, OP.mult, OP.add))

    def held(out, x):
        r = R("keep")
        op("v", [out], [x, r], lambda: g.vector.tensor_tensor_scan(ap(out), ap(r), ap(x), 0.0, OP.add, OP.max))

    def act(out, x, scale=1.0):
        op("a", [out], [x], lambda: g.scalar.activation(ap(out), ap(x), COPY, scale=scale))

    def act_pick(out, win, off):
        op("a", [out], [win, off], lambda: g.scalar.activation(ap(out), ap(win).indirect(ap(off)), COPY))

    def quant(q, x, a=0, b=None):
        o, s = R(q, a, b), R(q + "s", a, b)
        op("v", [o, s], [x], lambda: g.vector.quantize_mx(ap(o), ap(s), ap(x)))

    def mm(bank, l, la, r, ra, rb):
        o = R("p%d" % bank, 0, rb - ra)
        ops = [R(l, la, la + 128), R(l + "s", la, la + 128), R(r, ra, rb), R(r + "s", ra, rb)]
        op("t", [o], ops, lambda: g.tensor.matmul_mx(ap(o), ap(ops[0]), ap(ops[1]), ap(ops[2]), ap(ops[3]), True, True))

    nd = [0]

    def dma(q, writes, reads, out, in_):
        sem = "d%d" % nd[0]
        nd[0] += 1
        op(q, writes, reads, lambda: Q[q].dma_start(out, in_), sem, 16)

    def lanes(src, dst):
        return topo.engines(src, dst)[:8]

    def send(dst, land, src, k, s, codes):
        e = lanes(core, dst)
        rid, pid, _ = topo.addr(dst)
        hazards("g", [src], [])
        o, i = T[land][:, 0:src[2] - src[1]], ap(src)
        if codes:
            o, i = o.bitcast(dt.uint8), i.bitcast(dt.uint8)
        g.remote_dma(out_ap=o, in_ap=i, remote_sem=T.sem["arr%s%d" % (k, s)], local_sem=T.sem["snt%s%d" % (k, s)],
                     pid=pid, routing_id=rid, dma_engine_mask=sum(1 << j for j in e))
        sem = "snt%s%d" % (k, s)
        cnt[sem] = len(e)
        note("g", [src], [], (sem, len(e)))

    def arrives(land, k, s, src):
        sem = "arr%s%d" % (k, s)
        cnt[sem] = len(lanes(src, core))
        note("g", [], [R(land)], (sem, cnt[sem]))

    dma("a", [R("ut")], [], T.ut[:, :], T.u[:, :])
    dma("s", [R("x0", 0, 4 * H)], [], T.x0[:, 0:4 * H], T.x[:, 0:4 * H])
    dma("s", [R("x0", 4 * H, 4 * C)], [], T.x0[:, 4 * H:4 * C], T.x[:, 4 * H:4 * C])
    dma("a", [R("mli")], [], T.mli[:, :], T.ml[:, :])
    dma("s", [R("wq")], [], T.wq[:, :].bitcast(dt.uint8), T.wc[:, :])
    dma("s", [R("wqs")], [], T.wqs[:, :], T.ws[:, :])
    dma("s", [R("vt")], [], T.vt[:, :], T.v[:, :])

    def iota(n, w, pattern, base, cm):
        r = R(n, 0, w)
        f = SCRATCH[n][2] == F32
        op("g", [r], [], lambda: g.iota(ap(r), pattern, base, cm, allow_small_or_imprecise_dtypes=True) if f
           else g.iota(ap(r), pattern, base, cm))

    iota("pi", 42, [[0, 42]], 0, 1)
    iota("fi", 16, [[1, 16]], 0, 0)
    iota("ui", 8, [[16, 8]], 0, 0)
    iota("io", 672, [[1, 672]], 0, 0)
    ts(R("pm"), R("pi"), 15, OP.bitwise_and)
    fill(R("ones"), 1.0)
    vcopy(R("pmu"), R("pm"))
    vcopy(R("pf"), R("pm", 0, 1))
    vcopy(R("up"), R("ui"))
    one = R("ones")
    for b in range(4):
        e = R("et", 512 * b, 512 * b + 512)
        op("g", [e], [one], lambda: g.affine_select(ap(e), ap(one), [[-1, 512]], OP.is_equal, 0.0, b, 4))
    pf, pf1, off = R("pf"), R("pf1"), R("off")
    ts(pf1, pf, 1.0, OP.add)
    ts(off, pf, 15.0, OP.is_lt, 2.0, OP.mult)
    tsp(R("ka"), R("fi"), pf, OP.is_le, -8.0, OP.mult)
    tsp(R("m1"), R("fi"), pf, OP.is_equal)
    tsp(R("kb"), R("fi"), pf1, OP.is_equal, 2.0, OP.mult)
    fill(R("rst"), 1.0)
    tt(R("k16"), R("ka"), R("kb"), OP.add)
    fill(R("rst", 0, H, 16), 0.0)
    act_pick(R("mask"), R("m1"), R("pmu", 0, 14))
    act_pick(R("keep"), R("k16"), R("pmu", 0, 14))
    mask1 = R("mask")

    quant("uq", R("ut"))
    upk, uqc, uq2 = R("up"), R("uq"), R("uq2")
    op("v", [uq2], [uqc, upk],
       lambda: g.vector.tensor_copy(ap(uq2).bitcast(dt.uint32), ap(uqc).bitcast(dt.uint32).indirect(ap(upk))))
    us, us2 = R("uqs"), R("uq2s")
    op("v", [us2], [us, upk], lambda: g.vector.tensor_copy(ap(us2), ap(us).indirect(ap(upk))))
    for w in ("w0", "w1"):
        act(R(w, H, 672), R("io", H, 672))
    act(R("raw", 0, H), R("io", H, C))
    act(R("raw", H, C), R("io", 0, H))
    act(R("wa", H, C), R("io", C, 672))
    act(R("wu", 0, H), R("io", 0, H))
    act(R("wf", H, C), R("io", H, C))

    def prep(m):
        ts(R("tt"), m, 224.0, OP.is_ge, 224.0, OP.mult)
        ts(R("sg"), R("tt"), -2.0, OP.mult, 224.0, OP.add)
        tt(R("mmf"), m, R("tt"), OP.subtract)
        tsp(R("os0"), R("sg"), off, OP.mult)
        vcopy(R("mm"), R("mmf"))
        tt(R("mf2"), m, R("os0"), OP.subtract)

    def plane(x, half, b):
        act(R("xp%d" % b, half * H, half * H + H), R(x, half * 4 * H + b, half * 4 * H + 4 * H, 4))

    def halfcols(x, half):
        return R(x, half * 4 * H, half * 4 * H + 4 * H)

    vcopy(R("mf"), R("mli"))
    quant("qx", halfcols("x0", 0), 0, H)
    mm(0, "uq2", 0, "qx", 0, H)
    plane("x0", 0, 0)
    plane("x0", 0, 1)
    act(R("sup"), R("p0", 0, H))
    quant("qx", halfcols("x0", 1), H, C)
    mm(1, "uq2", 0, "qx", H, C)
    prep(R("mf"))
    todo = [(0, 2), (0, 3)]

    for s in ROUNDS:
        last = s == ROUNDS[-1]
        xs, xn = "x%d" % (s - 1), "x%d" % s
        peer = T.cores[rank ^ s]
        land_b, land_q = "lb%d" % s, "lq%d" % s
        arrives(land_b, "b", s, peer)
        arrives(land_q, "q", s, peer)
        arrives(land_q + "s", "s", s, peer)

        tt(R("sw"), R("sup"), R("p1", 0, H), OP.is_gt)
        bu, sw, up = R("bu"), R("sw"), R("mm", 0, 14)
        op("v", [bu], [sw, up], lambda: g.vector.tensor_copy(ap(bu), ap(sw).indirect(ap(up))))
        act_pick(R("bl"), sw, R("mm", 14, 28))
        for half, b in todo + [(1, b) for b in range(4)]:
            plane(xs, half, b)
        todo = []
        held(R("sc", C, 672), sw)
        held(R("sc", 0, H), bu)
        held(R("sc", H, C), R("bl"))
        tsp(R("af"), R("sc", C + 15, 672, 16), off, OP.subtract)
        tt(R("rr"), R("sc", 15, C, 16), R("sg"), OP.mult)
        tt(R("qq"), R("rr"), R("mf2"), OP.add)
        tt(R("dd"), R("qq", 14, 28), R("qq", 0, 14), OP.subtract)
        tt(R("ee"), R("dd"), R("af"), OP.mult)
        tt(R("nn", 0, 14), R("qq", 0, 14), R("ee"), OP.add)
        tt(R("nn", 14, 28), R("qq", 14, 28), R("ee"), OP.subtract)
        vcopy(R("n16"), R("nn"))
        send(peer, land_b, R("n16"), "b", s, False)
        n_up, n_lo = R("n16", 0, 14), R("n16", 14, 28)
        b_up, b_lo = R(land_b, 0, 14), R(land_b, 14, 28)

        act_pick(R("wa", 0, H), R("raw"), n_lo)

        def z(half, b):
            pick_tt(R(("zu", "zl")[half], b, 4 * H, 4), R("xp%d" % b), (n_up, n_lo)[half],
                    R(xs, half * 4 * H + b, half * 4 * H + 4 * H, 4), OP.add)

        for b in range(4):
            z(1, b)
        z(0, 0)
        quant("qzl", R("zl"))
        for b in range(4):
            mm(2 + b, "wq", 128 * b, "qzl", 0, H)
            act(R("al", b, 4 * H, 4), R("p%d" % (2 + b), 0, H), 0.015625)
        for b in range(1, 4):
            z(0, b)
        quant("qzu", R("zu"))
        quant("qal", R("al"))
        send(peer, land_q, R("qal"), "q", s, True)
        send(peer, land_q + "s", R("qals"), "s", s, False)
        for b in range(4):
            k = (6, 7, 2, 3)[b]
            mm(k, "wq", 128 * b, "qzu", 0, H)
            act(R("au", b, 4 * H, 4), R("p%d" % k, 0, H), 0.015625)
        if s == 1:
            quant("eq", R("et"))
            quant("vq", R("vt"))

        gbuf = ("ga", "gb")
        lists = ("la", "lb")
        win, lst = R("wa"), b_up
        for k in range(7):
            gk, lk, wk = R(gbuf[k % 2]), R(lists[k % 2]), "w%d" % (k % 2)
            pick_tt(gk, win, lst, mask1, OP.mult)
            act_pick(R(wk, 0, H), win, lst)
            if k == 1:
                quant("qau", R("au"))
                for b in range(4):
                    mm(4 + b, "eq", 128 * b, "qau", 0, H)
            scan(R("sa"), gk)
            vcopy(lk, R("sa", 15, H, 16))
            if 1 < k < 6:
                act(R("bp%d" % (k - 2), 0, H), R("p%d" % (2 + k), 0, H))
            win, lst = R(wk), lk
        for b in range(4):
            mm(2 + b, "eq", 128 * b, land_q, 0, H)
        w_up = R("wu", H, C)
        op("v", [w_up], [win, lst],
           lambda: g.vector.tensor_scalar(ap(w_up), ap(win).indirect(ap(lst)), 224.0, None, OP.subtract))
        pick_tt(R("ga"), R("wu"), n_up, mask1, OP.mult)
        act_pick(R("wf", 0, H), R("wu"), n_lo)
        for b in range(4):
            act(R("bp%d" % b, H, C), R("p%d" % (2 + b), 0, H))

        def new(half, b):
            lo, hi = half * 4 * H + b, half * 4 * H + 4 * H
            pick_tt(R(xn, lo, hi, 4), R("bp%d" % b), R("m16", 14 * half, 14 * half + 14), R(xs, lo, hi, 4), OP.add)

        scan(R("sm", 0, H), R("ga"))
        vcopy(R("m16", 0, 14), R("sm", 15, H, 16))
        pick_tt(R("gb"), R("wf"), b_lo, mask1, OP.mult)
        new(0, 0)
        scan(R("sm", H, C), R("gb"))
        new(0, 1)
        vcopy(R("m16", 14, 28), R("sm", H + 15, C, 16))
        new(0, 2)
        new(0, 3)
        new(1, 0)
        for half in (0, 1):
            if half == 1:
                for b in range(1, 4):
                    new(1, b)
            c0, c1 = half * H, half * H + H
            quant("qx", halfcols(xn, half), c0, c1)
            if not last:
                mm(half, "uq2", 0, "qx", c0, c1)
                if half == 1:
                    prep(R("sm", 15, C, 16))
                else:
                    for b in range(4):
                        plane(xn, 0, b)
                    act(R("sup"), R("p0", 0, H))
            else:
                mm(half, "vq", 0, "qx", c0, c1)
                dma("s", [], [R("qx", c0, c1)], T.oc[:, 4 * c0:4 * c1], T.qx[:, c0:c1].bitcast(dt.uint8))
                if half == 0:
                    act_pick(R("mrow", 0, H), R("wu"), n_up)
                    act_pick(R("mrow", H, C), R("wf"), b_lo)
                    act(R("yo", 0, H), R("p0", 0, H))
                    dma("s", [], [R("mrow")], T.mo[:, :], T.mrow[0:128:16, :])
                    dma("s", [], [R("yo", 0, H)], T.y[:, 0:H], T.yo[:, 0:H])
                else:
                    vcopy(R("yo", H, C), R("p1", 0, H))
                    dma("a", [], [R("yo", H, C)], T.y[:, H:C], T.yo[:, H:C])
                    for k in range(4):
                        dma("s" if k < 2 else "a", [], [R("qxs")], T.osc[4 * k:4 * k + 4, :], T.qxs[32 * k:32 * k + 4, :])

    for sem in sorted(cnt):
        need("g", sem, cnt[sem])
